import numpy as np
import ml_dtypes


def mxq(x, axis, fmt="e4m3"):
    dtype, down = {"e4m3": (ml_dtypes.float8_e4m3fn, 7), "e5m2": (ml_dtypes.float8_e5m2, 14)}[fmt]
    v = np.moveaxis(np.asarray(x, np.float32).astype(ml_dtypes.bfloat16).astype(np.float64), axis, -1)
    blocks = v.reshape(v.shape[:-1] + (-1, 32))
    amax = np.abs(blocks).max(-1, keepdims=True)
    byte = np.maximum(np.where(amax > 0, np.frexp(amax)[1] - 1 + 127, 0) - down, 1)
    scale = np.exp2(byte - 127.0)
    codes = (blocks / scale).astype(np.float32).astype(dtype).astype(np.float64)
    return np.moveaxis((codes * scale).reshape(v.shape), -1, axis)


WIDE = False


def mx_kscale(k):
    if not WIDE:
        return np.ones(k)
    levels = np.array([10, -10, 5, -5, 0])
    if k % 512:
        return np.exp2(np.random.permutation(np.resize(levels, k // 32))).repeat(32)
    a = np.empty((k // 512, 16))
    for p in range(k // 512):
        a[p, :8] = np.random.permutation(np.resize(levels, 8))
        for g in range(8):
            far = levels[np.abs(levels - a[p, g]) >= 10]
            a[p, g + 8] = far[np.random.randint(len(far))]
    return np.exp2(a.ravel()).repeat(32)


def f64(x):
    return np.asarray(x).astype(np.float64)


def striped(idx):
    return np.tile(idx.reshape(-1, 16).T, (8, 1)).astype(np.uint16)


def unstriped(offs):
    return offs[:16].T.reshape(-1).astype(np.int64)


def pack_weight(w):
    k, n = w.shape
    w = f64(np.asarray(w, np.float32).astype(ml_dtypes.bfloat16)).reshape(k // 32, 32, n)
    amax = np.abs(w).max(1)
    byte = np.clip(np.where(amax > 0, np.frexp(amax)[1] - 1 + 127 - 7, 1), 1, 254)
    scaled = (w * np.exp2(127.0 - byte)[:, None, :]).reshape(k, n).astype(np.float32)
    words = np.ascontiguousarray(scaled.reshape(k // 512, 128, 4, n).transpose(0, 1, 3, 2)).astype(ml_dtypes.float8_e4m3fn).view(np.uint8)
    return words, np.ascontiguousarray(byte.astype(np.uint8).reshape(k // 512, 16, n))


def unpack_weight(words, scales):
    g, p, n, _ = words.shape
    vals = np.ascontiguousarray(words).view(ml_dtypes.float8_e4m3fn).astype(np.float64) * np.repeat(np.exp2(scales.astype(np.float64) - 127.0), 8, axis=1)[..., None]
    return vals.transpose(0, 1, 3, 2).reshape(g * 512, n)


K, T, S, V, U = 1024, 2048, 512, 512, 256


def setup_inputs():
    n = np.random.standard_normal
    s = mx_kscale(K)[:, None]
    packed_xT = pack_weight(n((K, T)) * s)
    return {
        "x_words": packed_xT[0],
        "x_scales": packed_xT[1],
        "hT": (n((K, V)) / np.sqrt(K) / s).astype(np.float32),
        "gT": (n((K, V)) / np.sqrt(K) / s).astype(np.float32),
        "offs": striped(np.random.permutation(T)[:S]),
        "win": striped(np.random.permutation(S)[:U]),
        "los": striped(np.random.permutation(S)[:U]),
    }


def reference(x_words, x_scales, hT, gT, offs, win, los):
    hTq = mxq(f64(hT), 0, "e4m3")
    xq = unpack_weight(x_words, x_scales)[:, unstriped(offs)]
    gTq = mxq(f64(gT), 0, "e4m3")
    z = gTq.T @ xq
    dd = (hTq.T @ xq) - z
    mm = dd[:, unstriped(win)] - dd[:, unstriped(los)]
    return (mm - 1.0) ** 2

@@ -1,0 +1,169 @@
+from contextlib import ExitStack
+
+import concourse.mybir as mybir
+
+F32 = mybir.dt.float32
+BF16 = mybir.dt.bfloat16
+I32 = mybir.dt.int32
+U32 = mybir.dt.uint32
+U16 = mybir.dt.uint16
+U8 = mybir.dt.uint8
+FP8X4 = mybir.dt.float8_e4m3fn_x4
+ACT = mybir.ActivationFunctionType
+ALU = mybir.AluOpType
+
+K, T, S, V, U = 1024, 2048, 512, 512, 256
+P = 128
+PACK = 4
+K_PASS = P * PACK
+PASSES = K // K_PASS
+TILES = V // P
+LAST = TILES - 1
+CHUNKS = 2 * PASSES
+EARLY = 2
+LAST_VECTOR_COLS = 64
+TAIL_PARTS = 1
+
+FLOPS = 2 * 2 * K * V * S
+
+
+def tile_picked_ydpo_ipo_p_kernel(tc, x_words, x_scales, hT, gT, offs, win, los, out):
+    nc = tc.nc
+    with ExitStack() as ctx:
+        keep = ctx.enter_context(tc.tile_pool(name="keep", bufs=1))
+        psum = ctx.enter_context(tc.psum_pool(name="psum", bufs=1))
+
+        offs_sb = keep.tile([P, S // 16], U16, name="offs_sb")
+        win_sb = keep.tile([P, U // 16], U16, name="win_sb")
+        los_sb = keep.tile([P, U // 16], U16, name="los_sb")
+        words = [keep.tile([P, T], I32, name=f"words{o}", align_bytes=64) for o in range(PASSES)]
+        scale_rows = keep.tile([P, T], U8, name="scale_rows", align_bytes=64)
+        x_codes = [keep.tile([P, S], U32, name=f"x_codes{o}", align_bytes=64) for o in range(PASSES)]
+        x_planes = keep.tile([P, S], U8, name="x_planes", align_bytes=64)
+        minus_one = keep.tile([P, 1], F32, name="minus_one")
+
+        nc.vector.memset(scale_rows[:].bitcast(I32), 0)
+        nc.vector.memset(minus_one[:], -1.0)
+
+        def load_words(o):
+            nc.sync.dma_start(words[o][:], x_words[o].rearrange("p n t -> p (n t)").bitcast(I32))
+
+        raw, grouped = {}, {}
+
+        def load_chunk(i, c):
+            o, src = c // 2, (hT, gT)[c % 2]
+            raw[i, c] = keep.tile([P, PACK, P], F32, name=f"raw{i}_{c}", tag=f"raw{i}_{c}", align_bytes=64)
+            rows = src[o * K_PASS : (o + 1) * K_PASS, i * P : (i + 1) * P]
+            nc.sync.dma_start(raw[i, c][:], rows.rearrange("(p j) w -> p j w", j=PACK))
+
+        nc.sync.dma_start(offs_sb[:], offs)
+        load_words(0)
+        for q in range(4):
+            nc.sync.dma_start(
+                scale_rows[32 * q : 32 * q + 4 * PASSES, :].bitcast(I32),
+                x_scales[:, 4 * q : 4 * q + 4, :].bitcast(I32),
+            )
+        for c in range(EARLY):
+            load_chunk(0, c)
+        load_words(1)
+        for c in range(EARLY, CHUNKS):
+            load_chunk(0, c)
+        nc.sync.dma_start(los_sb[:], los)
+        nc.sync.dma_start(win_sb[:], win)
+        for i in range(1, TILES):
+            for c in range(CHUNKS):
+                load_chunk(i, c)
+
+        def gather_words(o):
+            nc.vector.tensor_copy(x_codes[o][:], words[o][:].bitcast(U32).indirect(offs_sb[:]))
+
+        gather_words(0)
+        nc.vector.tensor_copy(x_planes[:], scale_rows[:].indirect(offs_sb[:]))
+
+        def views(i, c, c0, c1):
+            d = grouped[i, c][:, PACK * c0 : PACK * c1].rearrange("p (b w j) -> p b j w", w=4, j=PACK)
+            s = raw[i, c][:, :, c0:c1].rearrange("p j (b w) -> p b j w", w=4)
+            return d, s
+
+        def cast(i, c):
+            sign = (1.0, -1.0)[c % 2]
+            grouped[i, c] = keep.tile([P, K_PASS], BF16, name=f"grouped{i}_{c}", align_bytes=64)
+            on_vector = P if (c == 2 and i > 0) else (LAST_VECTOR_COLS if (i, c) == (LAST, CHUNKS - 1) else 0)
+            split = P - on_vector
+            if split > 0:
+                d, s = views(i, c, 0, split)
+                nc.scalar.activation(d, s, ACT.Copy, scale=sign)
+            if split < P:
+                d, s = views(i, c, split, P)
+                nc.vector.tensor_scalar(d, s, sign, None, ALU.mult)
+
+        banks, dds, margins, losses = {}, {}, [], {}
+
+        def front(i):
+            parts = 2 if i == LAST else 1
+            n = S // parts
+            banks[i] = [psum.tile([P, n], F32, name=f"acc{i}_{b}") for b in range(parts)]
+            for c in range(CHUNKS):
+                o = c // 2
+                if c == 2:
+                    if i == 0:
+                        gather_words(1)
+                    else:
+                        empty(i - 1)
+                cast(i, c)
+                codes = keep.tile([P, P], U32, name=f"codes{i}_{c}", align_bytes=64)
+                plane = keep.tile([P, P], U8, name=f"plane{i}_{c}", align_bytes=64)
+                nc.vector.quantize_mx(out=codes[:].bitcast(FP8X4), scales=plane[:], in_=grouped[i, c][:])
+                for b in range(parts):
+                    nc.tensor.matmul_mx(
+                        out=banks[i][b][:],
+                        lhsT=codes[:].bitcast(FP8X4),
+                        lhsT_scale=plane[:],
+                        rhs=x_codes[o][:, b * n : (b + 1) * n].bitcast(FP8X4),
+                        rhs_scale=x_planes[4 * o : P, b * n : (b + 1) * n],
+                        start=(c == 0),
+                        stop=(c == CHUNKS - 1),
+                    )
+
+        def empty(i):
+            n = S // len(banks[i])
+            tag = f"raw{i + 1}_1" if i < LAST else "dd_last"
+            dds[i] = keep.tile([P, S], F32, name=f"dd{i}", tag=tag, align_bytes=64)
+            nc.scalar.copy(dds[i][:, 0:n], banks[i][0][:])
+            if i == LAST:
+                nc.scalar.copy(dds[i][:, n:S], banks[i][1][:])
+
+        def half(i, h):
+            return raw[i, CHUNKS - 1][:, 2 * h : 2 * h + 2, :].rearrange("p j w -> p (j w)")
+
+        def back(i):
+            parts = TAIL_PARTS if i == LAST else 1
+            u = U // parts
+            rejected = keep.tile([P, U], F32, name=f"rejected{i}", align_bytes=64)
+            margin = half(i + 1, 0) if i < LAST else keep.tile([P, U], F32, name="margin_last", align_bytes=64)[:]
+            nc.vector.tensor_copy(rejected[:], dds[i][:].indirect(los_sb[:]))
+            for a in range(parts):
+                cols = slice(a * u, (a + 1) * u)
+                picked = dds[i][:].indirect(win_sb[:, a * u // 16 : (a + 1) * u // 16])
+                nc.vector.tensor_tensor(margin[:, cols], picked, rejected[:, cols], ALU.subtract)
+                margins.append((i, cols, margin))
+
+        def finish(i, cols, margin):
+            if i == 0:
+                loss = half(LAST, 1)
+            elif i == 1:
+                loss = grouped[LAST, CHUNKS - 1][:].bitcast(F32)
+            else:
+                loss = keep.tile([P, U], F32, name=f"loss{i}_{cols.start}", align_bytes=64)[:]
+            nc.scalar.activation(loss[:, cols], margin[:, cols], ACT.Square, bias=minus_one[:])
+            nc.sync.dma_start(out[i * P : (i + 1) * P, cols], loss[:, cols])
+            losses[i] = loss
+
+        front(0)
+        for i in range(1, TILES):
+            front(i)
+            back(i - 1)
+        empty(LAST)
+        back(LAST)
+        for item in margins:
+            finish(*item)

@@ -19,10 +19,8 @@ K_PASS = P * PACK
 PASSES = K // K_PASS
 TILES = V // P
 LAST = TILES - 1
-CHUNKS = 2 * PASSES
-EARLY = 2
-LAST_VECTOR_COLS = 64
-TAIL_PARTS = 1
+HALF = V // 2
+TAIL_PARTS = 2
 
 FLOPS = 2 * 2 * K * V * S
 
@@ -37,7 +35,7 @@ def tile_picked_ydpo_ipo_p_kernel(tc, x_words, x_scales, hT, gT, offs, win, los,
         win_sb = keep.tile([P, U // 16], U16, name="win_sb")
         los_sb = keep.tile([P, U // 16], U16, name="los_sb")
         words = [keep.tile([P, T], I32, name=f"words{o}", align_bytes=64) for o in range(PASSES)]
-        scale_rows = keep.tile([P, T], U8, name="scale_rows", align_bytes=64)
+        scale_rows = keep.tile([P, T], U8, name="scale_rows", tag="scale_rows", align_bytes=64)
         x_codes = [keep.tile([P, S], U32, name=f"x_codes{o}", align_bytes=64) for o in range(PASSES)]
         x_planes = keep.tile([P, S], U8, name="x_planes", align_bytes=64)
         minus_one = keep.tile([P, 1], F32, name="minus_one")
@@ -48,122 +46,142 @@ def tile_picked_ydpo_ipo_p_kernel(tc, x_words, x_scales, hT, gT, offs, win, los,
         def load_words(o):
             nc.sync.dma_start(words[o][:], x_words[o].rearrange("p n t -> p (n t)").bitcast(I32))
 
-        raw, grouped = {}, {}
+        def load_rows(name, src, o, c0, c1):
+            raw = keep.tile([P, PACK, c1 - c0], F32, name=name, tag=name, align_bytes=64)
+            rows = src[o * K_PASS : (o + 1) * K_PASS, c0:c1]
+            nc.sync.dma_start(raw[:], rows.rearrange("(p j) w -> p j w", j=PACK))
+            return raw
 
-        def load_chunk(i, c):
-            o, src = c // 2, (hT, gT)[c % 2]
-            raw[i, c] = keep.tile([P, PACK, P], F32, name=f"raw{i}_{c}", tag=f"raw{i}_{c}", align_bytes=64)
-            rows = src[o * K_PASS : (o + 1) * K_PASS, i * P : (i + 1) * P]
-            nc.sync.dma_start(raw[i, c][:], rows.rearrange("(p j) w -> p j w", j=PACK))
-
-        nc.sync.dma_start(offs_sb[:], offs)
-        load_words(0)
         for q in range(4):
-            nc.sync.dma_start(
+            nc.gpsimd.dma_start(
                 scale_rows[32 * q : 32 * q + 4 * PASSES, :].bitcast(I32),
                 x_scales[:, 4 * q : 4 * q + 4, :].bitcast(I32),
             )
-        for c in range(EARLY):
-            load_chunk(0, c)
+        nc.sync.dma_start(offs_sb[:], offs)
+        load_words(0)
+        h_raw = [load_rows(f"h{o}", hT, o, 0, V) for o in range(PASSES)]
         load_words(1)
-        for c in range(EARLY, CHUNKS):
-            load_chunk(0, c)
-        nc.sync.dma_start(los_sb[:], los)
-        nc.sync.dma_start(win_sb[:], win)
-        for i in range(1, TILES):
-            for c in range(CHUNKS):
-                load_chunk(i, c)
+        g_raw = {}
+        for i in range(TILES):
+            for o in range(PASSES):
+                g_raw[i, o] = load_rows(f"g{o}_{i}", gT, o, i * P, (i + 1) * P)
+            if i == 0:
+                nc.sync.dma_start(los_sb[:], los)
+                nc.sync.dma_start(win_sb[:], win)
 
-        def gather_words(o):
-            nc.vector.tensor_copy(x_codes[o][:], words[o][:].bitcast(U32).indirect(offs_sb[:]))
+        def gather_words(o, c0, c1):
+            picks = offs_sb[:, c0 // 16 : c1 // 16]
+            nc.vector.tensor_copy(x_codes[o][:, c0:c1], words[o][:].bitcast(U32).indirect(picks))
 
-        gather_words(0)
-        nc.vector.tensor_copy(x_planes[:], scale_rows[:].indirect(offs_sb[:]))
-
-        def views(i, c, c0, c1):
-            d = grouped[i, c][:, PACK * c0 : PACK * c1].rearrange("p (b w j) -> p b j w", w=4, j=PACK)
-            s = raw[i, c][:, :, c0:c1].rearrange("p j (b w) -> p b j w", w=4)
-            return d, s
-
-        def cast(i, c):
-            sign = (1.0, -1.0)[c % 2]
-            grouped[i, c] = keep.tile([P, K_PASS], BF16, name=f"grouped{i}_{c}", align_bytes=64)
-            on_vector = P if (c == 2 and i > 0) else (LAST_VECTOR_COLS if (i, c) == (LAST, CHUNKS - 1) else 0)
-            split = P - on_vector
-            if split > 0:
-                d, s = views(i, c, 0, split)
-                nc.scalar.activation(d, s, ACT.Copy, scale=sign)
-            if split < P:
-                d, s = views(i, c, split, P)
+        def cast(name, raw, c0, c1, sign, on_vector):
+            grouped = keep.tile([P, PACK * (c1 - c0)], BF16, name=name + "_bf16", tag=name + "_bf16", align_bytes=64)
+            d = grouped[:].rearrange("p (b w j) -> p b j w", w=4, j=PACK)
+            s = raw[:, :, c0:c1].rearrange("p j (b w) -> p b j w", w=4)
+            if on_vector:
                 nc.vector.tensor_scalar(d, s, sign, None, ALU.mult)
+            else:
+                nc.scalar.activation(d, s, ACT.Copy, scale=sign)
+            return grouped
 
-        banks, dds, margins, losses = {}, {}, [], {}
+        def quantize(name, grouped, codes_tag=None):
+            width = grouped.shape[1] // PACK
+            codes = keep.tile([P, width], U32, name=name + "_codes", tag=codes_tag or name + "_codes", align_bytes=64)
+            plane = keep.tile([P, width], U8, name=name + "_plane", align_bytes=64)
+            nc.vector.quantize_mx(out=codes[:].bitcast(FP8X4), scales=plane[:], in_=grouped[:])
+            return [(codes[:, c : c + P], plane[:, c : c + P]) for c in range(0, width, P)]
+
+        banks = []
+        for i in range(TILES):
+            parts = 2 if i == 0 else 1
+            n = S // parts
+            banks.append([(psum.tile([P, n], F32, name=f"acc{i}_{b}"), slice(b * n, (b + 1) * n)) for b in range(parts)])
+
+        def multiply(i, operand, o, start=False, stop=False):
+            codes, plane = operand
+            for bank, cols in banks[i]:
+                nc.tensor.matmul_mx(
+                    out=bank[:],
+                    lhsT=codes.bitcast(FP8X4),
+                    lhsT_scale=plane,
+                    rhs=x_codes[o][:, cols].bitcast(FP8X4),
+                    rhs_scale=x_planes[4 * o : P, cols],
+                    start=start,
+                    stop=stop,
+                )
+
+        gather_words(0, 0, S)
+        nc.vector.tensor_copy(x_planes[:], scale_rows[:].indirect(offs_sb[:]))
+        for u in range(2):
+            tag = "scale_rows" if u == 0 else None
+            for v, operand in enumerate(quantize(f"h0_{u}", cast(f"h0_{u}", h_raw[0], u * HALF, (u + 1) * HALF, 1.0, False), tag)):
+                multiply(2 * u + v, operand, 0, start=True)
+        h1 = quantize("h1_0", cast("h1_0", h_raw[1], 0, HALF, 1.0, True))
+        h1_late = cast("h1_1", h_raw[1], HALF, V, 1.0, False)
+        gather_words(1, 0, S)
+
+        dds, rejected, margins = {}, {}, {}
 
         def front(i):
-            parts = 2 if i == LAST else 1
-            n = S // parts
-            banks[i] = [psum.tile([P, n], F32, name=f"acc{i}_{b}") for b in range(parts)]
-            for c in range(CHUNKS):
-                o = c // 2
-                if c == 2:
-                    if i == 0:
-                        gather_words(1)
-                    else:
-                        empty(i - 1)
-                cast(i, c)
-                codes = keep.tile([P, P], U32, name=f"codes{i}_{c}", align_bytes=64)
-                plane = keep.tile([P, P], U8, name=f"plane{i}_{c}", align_bytes=64)
-                nc.vector.quantize_mx(out=codes[:].bitcast(FP8X4), scales=plane[:], in_=grouped[i, c][:])
-                for b in range(parts):
-                    nc.tensor.matmul_mx(
-                        out=banks[i][b][:],
-                        lhsT=codes[:].bitcast(FP8X4),
-                        lhsT_scale=plane[:],
-                        rhs=x_codes[o][:, b * n : (b + 1) * n].bitcast(FP8X4),
-                        rhs_scale=x_planes[4 * o : P, b * n : (b + 1) * n],
-                        start=(c == 0),
-                        stop=(c == CHUNKS - 1),
-                    )
+            if i != 2:
+                if i != 1:
+                    multiply(i, h1[i], 1)
+                (g,) = quantize(f"gq0_{i}", cast(f"gq0_{i}", g_raw[i, 0], 0, P, -1.0, False))
+                multiply(i, g, 0)
+                if i == 1:
+                    multiply(i, h1[i], 1)
+                (g,) = quantize(f"gq1_{i}", cast(f"gq1_{i}", g_raw[i, 1], 0, P, -1.0, i == 1))
+                multiply(i, g, 1, stop=True)
+                if i == 1:
+                    h1.extend(quantize("h1_1", h1_late, "g1_0"))
+            else:
+                multiply(i, h1[i], 1)
+                grouped = keep.tile([P, PASSES * K_PASS], BF16, name=f"gq{i}_bf16", tag=f"gq{i}_bf16", align_bytes=64)
+                for o in range(PASSES):
+                    d = grouped[:, o * K_PASS : (o + 1) * K_PASS].rearrange("p (b w j) -> p b j w", w=4, j=PACK)
+                    s = g_raw[i, o][:].rearrange("p j (b w) -> p b j w", w=4)
+                    nc.scalar.activation(d, s, ACT.Copy, scale=-1.0)
+                for o, g in enumerate(quantize(f"gq{i}", grouped)):
+                    multiply(i, g, o, stop=(o == PASSES - 1))
 
         def empty(i):
-            n = S // len(banks[i])
-            tag = f"raw{i + 1}_1" if i < LAST else "dd_last"
+            tag = f"g0_{i + 1}" if i < LAST else "dd_last"
             dds[i] = keep.tile([P, S], F32, name=f"dd{i}", tag=tag, align_bytes=64)
-            nc.scalar.copy(dds[i][:, 0:n], banks[i][0][:])
-            if i == LAST:
-                nc.scalar.copy(dds[i][:, n:S], banks[i][1][:])
+            for bank, cols in banks[i]:
+                nc.scalar.copy(dds[i][:, cols], bank[:])
 
-        def half(i, h):
-            return raw[i, CHUNKS - 1][:, 2 * h : 2 * h + 2, :].rearrange("p j w -> p (j w)")
+        u = U // 2
 
-        def back(i):
-            parts = TAIL_PARTS if i == LAST else 1
-            u = U // parts
-            rejected = keep.tile([P, U], F32, name=f"rejected{i}", align_bytes=64)
-            margin = half(i + 1, 0) if i < LAST else keep.tile([P, U], F32, name="margin_last", align_bytes=64)[:]
-            nc.vector.tensor_copy(rejected[:], dds[i][:].indirect(los_sb[:]))
-            for a in range(parts):
+        def fetch_rejected(i):
+            rejected[i] = keep.tile([P, U], F32, name=f"rejected{i}", tag=f"rejected{i}", align_bytes=64)
+            for a in range(2):
+                picked = dds[i][:].indirect(los_sb[:, a * u // 16 : (a + 1) * u // 16])
+                nc.vector.tensor_copy(rejected[i][:, a * u : (a + 1) * u], picked)
+
+        def fetch_margin(i):
+            tag = f"g1_{i + 2}" if (i == 1) else f"margin{i}"
+            margins[i] = keep.tile([P, U], F32, name=f"margin{i}", tag=tag, align_bytes=64)[:]
+            for a in range(2):
                 cols = slice(a * u, (a + 1) * u)
                 picked = dds[i][:].indirect(win_sb[:, a * u // 16 : (a + 1) * u // 16])
-                nc.vector.tensor_tensor(margin[:, cols], picked, rejected[:, cols], ALU.subtract)
-                margins.append((i, cols, margin))
-
-        def finish(i, cols, margin):
-            if i == 0:
-                loss = half(LAST, 1)
-            elif i == 1:
-                loss = grouped[LAST, CHUNKS - 1][:].bitcast(F32)
-            else:
-                loss = keep.tile([P, U], F32, name=f"loss{i}_{cols.start}", align_bytes=64)[:]
-            nc.scalar.activation(loss[:, cols], margin[:, cols], ACT.Square, bias=minus_one[:])
-            nc.sync.dma_start(out[i * P : (i + 1) * P, cols], loss[:, cols])
-            losses[i] = loss
+                nc.vector.tensor_tensor(margins[i][:, cols], picked, rejected[i][:, cols], ALU.subtract)
 
         front(0)
-        for i in range(1, TILES):
-            front(i)
-            back(i - 1)
-        empty(LAST)
-        back(LAST)
-        for item in margins:
-            finish(*item)
+        front(1)
+        empty(0)
+        for i in range(TILES):
+            fetch_rejected(i)
+            if i + 2 < TILES:
+                front(i + 2)
+            fetch_margin(i)
+            if i < LAST:
+                empty(i + 1)
+
+        loss_tags = [f"gq1_{LAST}_bf16", "rejected2", "loss2", "loss3"]
+        for i in range(TILES):
+            parts = 2 if i == LAST else 1
+            n = U // parts
+            loss = keep.tile([P, U], F32, name=f"loss{i}", tag=loss_tags[i], align_bytes=64)[:]
+            for a in range(parts):
+                cols = slice(a * n, (a + 1) * n)
+                nc.scalar.activation(loss[:, cols], margins[i][:, cols], ACT.Square, bias=minus_one[:])
+                nc.sync.dma_start(out[i * P : (i + 1) * P, cols], loss[:, cols])

@@ -20,7 +20,11 @@ PASSES = K // K_PASS
 TILES = V // P
 LAST = TILES - 1
 HALF = V // 2
-TAIL_PARTS = 2
+QUADRANTS, QUADRANT = 4, 32
+PLANE_ROWS = 4
+PER_COLUMN = 16
+RUN = 2
+PAIR_PART = U // 2
 
 FLOPS = 2 * 2 * K * V * S
 
@@ -31,9 +35,9 @@ def tile_picked_ydpo_ipo_p_kernel(tc, x_words, x_scales, hT, gT, offs, win, los,
         keep = ctx.enter_context(tc.tile_pool(name="keep", bufs=1))
         psum = ctx.enter_context(tc.psum_pool(name="psum", bufs=1))
 
-        offs_sb = keep.tile([P, S // 16], U16, name="offs_sb")
-        win_sb = keep.tile([P, U // 16], U16, name="win_sb")
-        los_sb = keep.tile([P, U // 16], U16, name="los_sb")
+        offs_sb = keep.tile([P, S // PER_COLUMN], U16, name="offs_sb")
+        win_sb = keep.tile([P, U // PER_COLUMN], U16, name="win_sb")
+        los_sb = keep.tile([P, U // PER_COLUMN], U16, name="los_sb")
         words = [keep.tile([P, T], I32, name=f"words{o}", align_bytes=64) for o in range(PASSES)]
         scale_rows = keep.tile([P, T], U8, name="scale_rows", tag="scale_rows", align_bytes=64)
         x_codes = [keep.tile([P, S], U32, name=f"x_codes{o}", align_bytes=64) for o in range(PASSES)]
@@ -52,13 +56,13 @@ def tile_picked_ydpo_ipo_p_kernel(tc, x_words, x_scales, hT, gT, offs, win, los,
             nc.sync.dma_start(raw[:], rows.rearrange("(p j) w -> p j w", j=PACK))
             return raw
 
-        for q in range(4):
+        for q in range(QUADRANTS):
             nc.gpsimd.dma_start(
-                scale_rows[32 * q : 32 * q + 4 * PASSES, :].bitcast(I32),
-                x_scales[:, 4 * q : 4 * q + 4, :].bitcast(I32),
+                scale_rows[QUADRANT * q : QUADRANT * q + PLANE_ROWS * PASSES, :].bitcast(I32),
+                x_scales[:, PLANE_ROWS * q : PLANE_ROWS * (q + 1), :].bitcast(I32),
             )
-        nc.sync.dma_start(offs_sb[:], offs)
         load_words(0)
+        nc.sync.dma_start(offs_sb[:], offs)
         h_raw = [load_rows(f"h{o}", hT, o, 0, V) for o in range(PASSES)]
         load_words(1)
         g_raw = {}
@@ -69,18 +73,20 @@ def tile_picked_ydpo_ipo_p_kernel(tc, x_words, x_scales, hT, gT, offs, win, los,
                 nc.sync.dma_start(los_sb[:], los)
                 nc.sync.dma_start(win_sb[:], win)
 
-        def gather_words(o, c0, c1):
-            picks = offs_sb[:, c0 // 16 : c1 // 16]
-            nc.vector.tensor_copy(x_codes[o][:, c0:c1], words[o][:].bitcast(U32).indirect(picks))
+        def gather_words(o):
+            nc.vector.tensor_copy(x_codes[o][:], words[o][:].bitcast(U32).indirect(offs_sb[:]))
 
-        def cast(name, raw, c0, c1, sign, on_vector):
-            grouped = keep.tile([P, PACK * (c1 - c0)], BF16, name=name + "_bf16", tag=name + "_bf16", align_bytes=64)
-            d = grouped[:].rearrange("p (b w j) -> p b j w", w=4, j=PACK)
-            s = raw[:, :, c0:c1].rearrange("p j (b w) -> p b j w", w=4)
+        def cast_into(grouped, raw, sign, on_vector=False):
+            dst = grouped.rearrange("p (b w j) -> p b j w", w=RUN, j=PACK)
+            src = raw.rearrange("p j (b w) -> p b j w", w=RUN)
             if on_vector:
-                nc.vector.tensor_scalar(d, s, sign, None, ALU.mult)
+                nc.vector.tensor_scalar(dst, src, sign, None, ALU.mult)
             else:
-                nc.scalar.activation(d, s, ACT.Copy, scale=sign)
+                nc.scalar.activation(dst, src, ACT.Copy, scale=sign)
+
+        def cast(name, raw, sign, on_vector=False):
+            grouped = keep.tile([P, PACK * raw.shape[2]], BF16, name=name + "_bf16", tag=name + "_bf16", align_bytes=64)
+            cast_into(grouped[:], raw, sign, on_vector)
             return grouped
 
         def quantize(name, grouped, codes_tag=None):
@@ -92,9 +98,8 @@ def tile_picked_ydpo_ipo_p_kernel(tc, x_words, x_scales, hT, gT, offs, win, los,
 
         banks = []
         for i in range(TILES):
-            parts = 2 if i == 0 else 1
-            n = S // parts
-            banks.append([(psum.tile([P, n], F32, name=f"acc{i}_{b}"), slice(b * n, (b + 1) * n)) for b in range(parts)])
+            n = S // 2 if i == 0 else S
+            banks.append([(psum.tile([P, n], F32, name=f"acc{i}_{c // n}"), slice(c, c + n)) for c in range(0, S, n)])
 
         def multiply(i, operand, o, start=False, stop=False):
             codes, plane = operand
@@ -104,44 +109,45 @@ def tile_picked_ydpo_ipo_p_kernel(tc, x_words, x_scales, hT, gT, offs, win, los,
                     lhsT=codes.bitcast(FP8X4),
                     lhsT_scale=plane,
                     rhs=x_codes[o][:, cols].bitcast(FP8X4),
-                    rhs_scale=x_planes[4 * o : P, cols],
+                    rhs_scale=x_planes[PLANE_ROWS * o : P, cols],
                     start=start,
                     stop=stop,
                 )
 
-        gather_words(0, 0, S)
+        gather_words(0)
         nc.vector.tensor_copy(x_planes[:], scale_rows[:].indirect(offs_sb[:]))
-        for u in range(2):
-            tag = "scale_rows" if u == 0 else None
-            for v, operand in enumerate(quantize(f"h0_{u}", cast(f"h0_{u}", h_raw[0], u * HALF, (u + 1) * HALF, 1.0, False), tag)):
-                multiply(2 * u + v, operand, 0, start=True)
-        h1 = quantize("h1_0", cast("h1_0", h_raw[1], 0, HALF, 1.0, True))
-        h1_late = cast("h1_1", h_raw[1], HALF, V, 1.0, False)
-        gather_words(1, 0, S)
+        for half in range(2):
+            grouped = cast(f"h0_{half}", h_raw[0][:, :, half * HALF : (half + 1) * HALF], 1.0)
+            operands = quantize(f"h0_{half}", grouped, "scale_rows" if half == 0 else None)
+            for n, operand in enumerate(operands):
+                multiply(2 * half + n, operand, 0, start=True)
+        h1 = quantize("h1_0", cast("h1_0", h_raw[1][:, :, 0:HALF], 1.0, on_vector=True))
+        h1_second_half = cast("h1_1", h_raw[1][:, :, HALF:V], 1.0)
+        gather_words(1)
 
         dds, rejected, margins = {}, {}, {}
 
-        def front(i):
-            if i != 2:
-                if i != 1:
-                    multiply(i, h1[i], 1)
-                (g,) = quantize(f"gq0_{i}", cast(f"gq0_{i}", g_raw[i, 0], 0, P, -1.0, False))
-                multiply(i, g, 0)
-                if i == 1:
-                    multiply(i, h1[i], 1)
-                (g,) = quantize(f"gq1_{i}", cast(f"gq1_{i}", g_raw[i, 1], 0, P, -1.0, i == 1))
-                multiply(i, g, 1, stop=True)
-                if i == 1:
-                    h1.extend(quantize("h1_1", h1_late, "g1_0"))
-            else:
+        def g_pass(i, o, on_vector=False):
+            (operand,) = quantize(f"gq{o}_{i}", cast(f"gq{o}_{i}", g_raw[i, o][:], -1.0, on_vector))
+            multiply(i, operand, o, stop=(o == PASSES - 1))
+
+        def g_passes(i):
+            if i == 1:
+                g_pass(i, 0)
+                multiply(i, h1[i], 1)
+                g_pass(i, 1, on_vector=True)
+                h1.extend(quantize("h1_1", h1_second_half, "g1_0"))
+            elif i == 2:
                 multiply(i, h1[i], 1)
                 grouped = keep.tile([P, PASSES * K_PASS], BF16, name=f"gq{i}_bf16", tag=f"gq{i}_bf16", align_bytes=64)
                 for o in range(PASSES):
-                    d = grouped[:, o * K_PASS : (o + 1) * K_PASS].rearrange("p (b w j) -> p b j w", w=4, j=PACK)
-                    s = g_raw[i, o][:].rearrange("p j (b w) -> p b j w", w=4)
-                    nc.scalar.activation(d, s, ACT.Copy, scale=-1.0)
-                for o, g in enumerate(quantize(f"gq{i}", grouped)):
-                    multiply(i, g, o, stop=(o == PASSES - 1))
+                    cast_into(grouped[:, o * K_PASS : (o + 1) * K_PASS], g_raw[i, o][:], -1.0)
+                for o, operand in enumerate(quantize(f"gq{i}", grouped)):
+                    multiply(i, operand, o, stop=(o == PASSES - 1))
+            else:
+                multiply(i, h1[i], 1)
+                for o in range(PASSES):
+                    g_pass(i, o)
 
         def empty(i):
             tag = f"g0_{i + 1}" if i < LAST else "dd_last"
@@ -149,39 +155,37 @@ def tile_picked_ydpo_ipo_p_kernel(tc, x_words, x_scales, hT, gT, offs, win, los,
             for bank, cols in banks[i]:
                 nc.scalar.copy(dds[i][:, cols], bank[:])
 
-        u = U // 2
+        def picked(i, pair_list, c):
+            return dds[i][:].indirect(pair_list[:, c // PER_COLUMN : (c + PAIR_PART) // PER_COLUMN])
 
         def fetch_rejected(i):
             rejected[i] = keep.tile([P, U], F32, name=f"rejected{i}", tag=f"rejected{i}", align_bytes=64)
-            for a in range(2):
-                picked = dds[i][:].indirect(los_sb[:, a * u // 16 : (a + 1) * u // 16])
-                nc.vector.tensor_copy(rejected[i][:, a * u : (a + 1) * u], picked)
+            for c in range(0, U, PAIR_PART):
+                nc.vector.tensor_copy(rejected[i][:, c : c + PAIR_PART], picked(i, los_sb, c))
 
         def fetch_margin(i):
-            tag = f"g1_{i + 2}" if (i == 1) else f"margin{i}"
-            margins[i] = keep.tile([P, U], F32, name=f"margin{i}", tag=tag, align_bytes=64)[:]
-            for a in range(2):
-                cols = slice(a * u, (a + 1) * u)
-                picked = dds[i][:].indirect(win_sb[:, a * u // 16 : (a + 1) * u // 16])
-                nc.vector.tensor_tensor(margins[i][:, cols], picked, rejected[i][:, cols], ALU.subtract)
+            tag = f"g1_{LAST}" if i == 1 else f"margin{i}"
+            margins[i] = keep.tile([P, U], F32, name=f"margin{i}", tag=tag, align_bytes=64)
+            for c in range(0, U, PAIR_PART):
+                cols = slice(c, c + PAIR_PART)
+                nc.vector.tensor_tensor(margins[i][:, cols], picked(i, win_sb, c), rejected[i][:, cols], ALU.subtract)
 
-        front(0)
-        front(1)
+        g_passes(0)
+        g_passes(1)
         empty(0)
         for i in range(TILES):
             fetch_rejected(i)
             if i + 2 < TILES:
-                front(i + 2)
+                g_passes(i + 2)
             fetch_margin(i)
             if i < LAST:
                 empty(i + 1)
 
         loss_tags = [f"gq1_{LAST}_bf16", "rejected2", "loss2", "loss3"]
         for i in range(TILES):
-            parts = 2 if i == LAST else 1
-            n = U // parts
-            loss = keep.tile([P, U], F32, name=f"loss{i}", tag=loss_tags[i], align_bytes=64)[:]
-            for a in range(parts):
-                cols = slice(a * n, (a + 1) * n)
+            n = PAIR_PART if i == LAST else U
+            loss = keep.tile([P, U], F32, name=f"loss{i}", tag=loss_tags[i], align_bytes=64)
+            for c in range(0, U, n):
+                cols = slice(c, c + n)
                 nc.scalar.activation(loss[:, cols], margins[i][:, cols], ACT.Square, bias=minus_one[:])
                 nc.sync.dma_start(out[i * P : (i + 1) * P, cols], loss[:, cols])

from contextlib import ExitStack

import concourse.mybir as mybir

F32 = mybir.dt.float32
BF16 = mybir.dt.bfloat16
I32 = mybir.dt.int32
U32 = mybir.dt.uint32
U16 = mybir.dt.uint16
U8 = mybir.dt.uint8
FP8X4 = mybir.dt.float8_e4m3fn_x4
ACT = mybir.ActivationFunctionType
ALU = mybir.AluOpType

K, T, S, V, U = 1024, 2048, 512, 512, 256
P = 128
PACK = 4
K_PASS = P * PACK
PASSES = K // K_PASS
TILES = V // P
LAST = TILES - 1
HALF = V // 2
QUADRANTS, QUADRANT = 4, 32
PLANE_ROWS = 4
PER_COLUMN = 16
RUN = 2
PAIR_PART = U // 2

FLOPS = 2 * 2 * K * V * S


def tile_picked_ydpo_ipo_p_kernel(tc, x_words, x_scales, hT, gT, offs, win, los, out):
    nc = tc.nc
    with ExitStack() as ctx:
        keep = ctx.enter_context(tc.tile_pool(name="keep", bufs=1))
        psum = ctx.enter_context(tc.psum_pool(name="psum", bufs=1))

        offs_sb = keep.tile([P, S // PER_COLUMN], U16, name="offs_sb")
        win_sb = keep.tile([P, U // PER_COLUMN], U16, name="win_sb")
        los_sb = keep.tile([P, U // PER_COLUMN], U16, name="los_sb")
        words = [keep.tile([P, T], I32, name=f"words{o}", align_bytes=64) for o in range(PASSES)]
        scale_rows = keep.tile([P, T], U8, name="scale_rows", tag="scale_rows", align_bytes=64)
        x_codes = [keep.tile([P, S], U32, name=f"x_codes{o}", align_bytes=64) for o in range(PASSES)]
        x_planes = keep.tile([P, S], U8, name="x_planes", align_bytes=64)
        minus_one = keep.tile([P, 1], F32, name="minus_one")

        nc.vector.memset(scale_rows[:].bitcast(I32), 0)
        nc.vector.memset(minus_one[:], -1.0)

        def load_words(o):
            nc.sync.dma_start(words[o][:], x_words[o].rearrange("p n t -> p (n t)").bitcast(I32))

        def load_rows(name, src, o, c0, c1):
            raw = keep.tile([P, PACK, c1 - c0], F32, name=name, tag=name, align_bytes=64)
            rows = src[o * K_PASS : (o + 1) * K_PASS, c0:c1]
            nc.sync.dma_start(raw[:], rows.rearrange("(p j) w -> p j w", j=PACK))
            return raw

        for q in range(QUADRANTS):
            nc.gpsimd.dma_start(
                scale_rows[QUADRANT * q : QUADRANT * q + PLANE_ROWS * PASSES, :].bitcast(I32),
                x_scales[:, PLANE_ROWS * q : PLANE_ROWS * (q + 1), :].bitcast(I32),
            )
        load_words(0)
        nc.sync.dma_start(offs_sb[:], offs)
        h_raw = [load_rows(f"h{o}", hT, o, 0, V) for o in range(PASSES)]
        load_words(1)
        g_raw = {}
        for i in range(TILES):
            for o in range(PASSES):
                g_raw[i, o] = load_rows(f"g{o}_{i}", gT, o, i * P, (i + 1) * P)
            if i == 0:
                nc.sync.dma_start(los_sb[:], los)
                nc.sync.dma_start(win_sb[:], win)

        def gather_words(o):
            nc.vector.tensor_copy(x_codes[o][:], words[o][:].bitcast(U32).indirect(offs_sb[:]))

        def cast_into(grouped, raw, sign, on_vector=False):
            dst = grouped.rearrange("p (b w j) -> p b j w", w=RUN, j=PACK)
            src = raw.rearrange("p j (b w) -> p b j w", w=RUN)
            if on_vector:
                nc.vector.tensor_scalar(dst, src, sign, None, ALU.mult)
            else:
                nc.scalar.activation(dst, src, ACT.Copy, scale=sign)

        def cast(name, raw, sign, on_vector=False):
            grouped = keep.tile([P, PACK * raw.shape[2]], BF16, name=name + "_bf16", tag=name + "_bf16", align_bytes=64)
            cast_into(grouped[:], raw, sign, on_vector)
            return grouped

        def quantize(name, grouped, codes_tag=None):
            width = grouped.shape[1] // PACK
            codes = keep.tile([P, width], U32, name=name + "_codes", tag=codes_tag or name + "_codes", align_bytes=64)
            plane = keep.tile([P, width], U8, name=name + "_plane", align_bytes=64)
            nc.vector.quantize_mx(out=codes[:].bitcast(FP8X4), scales=plane[:], in_=grouped[:])
            return [(codes[:, c : c + P], plane[:, c : c + P]) for c in range(0, width, P)]

        banks = []
        for i in range(TILES):
            n = S // 2 if i == 0 else S
            banks.append([(psum.tile([P, n], F32, name=f"acc{i}_{c // n}"), slice(c, c + n)) for c in range(0, S, n)])

        def multiply(i, operand, o, start=False, stop=False):
            codes, plane = operand
            for bank, cols in banks[i]:
                nc.tensor.matmul_mx(
                    out=bank[:],
                    lhsT=codes.bitcast(FP8X4),
                    lhsT_scale=plane,
                    rhs=x_codes[o][:, cols].bitcast(FP8X4),
                    rhs_scale=x_planes[PLANE_ROWS * o : P, cols],
                    start=start,
                    stop=stop,
                )

        gather_words(0)
        nc.vector.tensor_copy(x_planes[:], scale_rows[:].indirect(offs_sb[:]))
        for half in range(2):
            grouped = cast(f"h0_{half}", h_raw[0][:, :, half * HALF : (half + 1) * HALF], 1.0)
            operands = quantize(f"h0_{half}", grouped, "scale_rows" if half == 0 else None)
            for n, operand in enumerate(operands):
                multiply(2 * half + n, operand, 0, start=True)
        h1 = quantize("h1_0", cast("h1_0", h_raw[1][:, :, 0:HALF], 1.0, on_vector=True))
        h1_second_half = cast("h1_1", h_raw[1][:, :, HALF:V], 1.0)
        gather_words(1)

        dds, rejected, margins = {}, {}, {}

        def g_pass(i, o, on_vector=False):
            (operand,) = quantize(f"gq{o}_{i}", cast(f"gq{o}_{i}", g_raw[i, o][:], -1.0, on_vector))
            multiply(i, operand, o, stop=(o == PASSES - 1))

        def g_passes(i):
            if i == 1:
                g_pass(i, 0)
                multiply(i, h1[i], 1)
                g_pass(i, 1, on_vector=True)
                h1.extend(quantize("h1_1", h1_second_half, "g1_0"))
            elif i == 2:
                multiply(i, h1[i], 1)
                grouped = keep.tile([P, PASSES * K_PASS], BF16, name=f"gq{i}_bf16", tag=f"gq{i}_bf16", align_bytes=64)
                for o in range(PASSES):
                    cast_into(grouped[:, o * K_PASS : (o + 1) * K_PASS], g_raw[i, o][:], -1.0)
                for o, operand in enumerate(quantize(f"gq{i}", grouped)):
                    multiply(i, operand, o, stop=(o == PASSES - 1))
            else:
                multiply(i, h1[i], 1)
                for o in range(PASSES):
                    g_pass(i, o)

        def empty(i):
            tag = f"g0_{i + 1}" if i < LAST else "dd_last"
            dds[i] = keep.tile([P, S], F32, name=f"dd{i}", tag=tag, align_bytes=64)
            for bank, cols in banks[i]:
                nc.scalar.copy(dds[i][:, cols], bank[:])

        def picked(i, pair_list, c):
            return dds[i][:].indirect(pair_list[:, c // PER_COLUMN : (c + PAIR_PART) // PER_COLUMN])

        def fetch_rejected(i):
            rejected[i] = keep.tile([P, U], F32, name=f"rejected{i}", tag=f"rejected{i}", align_bytes=64)
            for c in range(0, U, PAIR_PART):
                nc.vector.tensor_copy(rejected[i][:, c : c + PAIR_PART], picked(i, los_sb, c))

        def fetch_margin(i):
            tag = f"g1_{LAST}" if i == 1 else f"margin{i}"
            margins[i] = keep.tile([P, U], F32, name=f"margin{i}", tag=tag, align_bytes=64)
            for c in range(0, U, PAIR_PART):
                cols = slice(c, c + PAIR_PART)
                nc.vector.tensor_tensor(margins[i][:, cols], picked(i, win_sb, c), rejected[i][:, cols], ALU.subtract)

        g_passes(0)
        g_passes(1)
        empty(0)
        for i in range(TILES):
            fetch_rejected(i)
            if i + 2 < TILES:
                g_passes(i + 2)
            fetch_margin(i)
            if i < LAST:
                empty(i + 1)

        loss_tags = [f"gq1_{LAST}_bf16", "rejected2", "loss2", "loss3"]
        for i in range(TILES):
            n = PAIR_PART if i == LAST else U
            loss = keep.tile([P, U], F32, name=f"loss{i}", tag=loss_tags[i], align_bytes=64)
            for c in range(0, U, n):
                cols = slice(c, c + n)
                nc.scalar.activation(loss[:, cols], margins[i][:, cols], ACT.Square, bias=minus_one[:])
                nc.sync.dma_start(out[i * P : (i + 1) * P, cols], loss[:, cols])
